import numpy as np
import ml_dtypes


def mxq(x, axis, fmt="e4m3"):
    dtype, down = {"e4m3": (ml_dtypes.float8_e4m3fn, 7), "e5m2": (ml_dtypes.float8_e5m2, 14)}[fmt]
    v = np.moveaxis(np.asarray(x, np.float32).astype(ml_dtypes.bfloat16).astype(np.float64), axis, -1)
    blocks = v.reshape(v.shape[:-1] + (-1, 32))
    amax = np.abs(blocks).max(-1, keepdims=True)
    byte = np.maximum(np.where(amax > 0, np.frexp(amax)[1] - 1 + 127, 0) - down, 1)
    scale = np.exp2(byte - 127.0)
    codes = (blocks / scale).astype(np.float32).astype(dtype).astype(np.float64)
    return np.moveaxis((codes * scale).reshape(v.shape), -1, axis)


WIDE = False


def mx_kscale(k):
    if not WIDE:
        return np.ones(k)
    levels = np.array([10, -10, 5, -5, 0])
    if k % 512:
        return np.exp2(np.random.permutation(np.resize(levels, k // 32))).repeat(32)
    a = np.empty((k // 512, 16))
    for p in range(k // 512):
        a[p, :8] = np.random.permutation(np.resize(levels, 8))
        for g in range(8):
            far = levels[np.abs(levels - a[p, g]) >= 10]
            a[p, g + 8] = far[np.random.randint(len(far))]
    return np.exp2(a.ravel()).repeat(32)


def f64(x):
    return np.asarray(x).astype(np.float64)


def striped(idx):
    return np.tile(idx.reshape(-1, 16).T, (8, 1)).astype(np.uint16)


def unstriped(offs):
    return offs[:16].T.reshape(-1).astype(np.int64)


def striped8(idx):
    return np.concatenate([x.reshape(-1, 16).T for x in idx]).astype(np.uint16)


def runs(offs, k):
    lists = np.stack([offs[16 * r : 16 * r + 16].T.reshape(-1) for r in range(8)]).astype(np.int64)
    return lists[np.arange(k) % 512 // 64]


def pack_weight(w):
    k, n = w.shape
    w = f64(np.asarray(w, np.float32).astype(ml_dtypes.bfloat16)).reshape(k // 32, 32, n)
    amax = np.abs(w).max(1)
    byte = np.clip(np.where(amax > 0, np.frexp(amax)[1] - 1 + 127 - 7, 1), 1, 254)
    scaled = (w * np.exp2(127.0 - byte)[:, None, :]).reshape(k, n).astype(np.float32)
    words = np.ascontiguousarray(scaled.reshape(k // 512, 128, 4, n).transpose(0, 1, 3, 2)).astype(ml_dtypes.float8_e4m3fn).view(np.uint8)
    return words, np.ascontiguousarray(byte.astype(np.uint8).reshape(k // 512, 16, n))


def unpack_weight(words, scales):
    g, p, n, _ = words.shape
    vals = np.ascontiguousarray(words).view(ml_dtypes.float8_e4m3fn).astype(np.float64) * np.repeat(np.exp2(scales.astype(np.float64) - 127.0), 8, axis=1)[..., None]
    return vals.transpose(0, 1, 3, 2).reshape(g * 512, n)


K, T, S, N, H, W = 512, 2048, 512, 512, 512, 256


def setup_inputs():
    n = np.random.standard_normal
    s = mx_kscale(K)[:, None]
    u = mx_kscale(H)
    packed_xT = pack_weight(n((K, T)) * s)
    perm = np.stack([np.random.permutation(S) for _ in range(8)])
    return {
        "x_words": packed_xT[0],
        "x_scales": packed_xT[1],
        "w1": (n((K, H)) / np.sqrt(K) / s).astype(np.float32),
        "gn": (np.random.uniform(0.5, 1.5, (H, 1)) * u[:, None]).astype(np.float32),
        "w2": (n((H, N)) / np.sqrt(H) / u[:, None]).astype(np.float32),
        "offs": striped(np.random.permutation(T)[:S]),
        "n1": striped8(perm[:, :W]),
        "n2": striped8(perm[:, W:]),
        "n3": striped8(np.stack([np.random.permutation(S) for _ in range(8)])),
        "n4": striped8(np.stack([np.random.permutation(S) for _ in range(8)])),
        "n5": striped8(np.stack([np.random.permutation(S) for _ in range(8)])),
    }


def reference(x_words, x_scales, w1, gn, w2, offs, n1, n2, n3, n4, n5):
    xq = unpack_weight(x_words, x_scales)[:, unstriped(offs)]
    y = mxq(f64(w1), 0, "e4m3").T @ xq
    pa = y[np.arange(H)[:, None], runs(n1, H)]
    pb = y[np.arange(H)[:, None], runs(n2, H)]
    ra = pa - (0.5 * pb)
    ds = y.copy()
    ds[np.arange(H)[:, None], runs(n2, H)] = ra
    z = f64(gn) * (ds - (0.5 * (ds[np.arange(H)[:, None], runs(n3, H)])))
    h = mxq(f64(w2), 0, "e4m3").T @ mxq(z, 0, "e4m3")
    return np.maximum(h, y[np.arange(H)[:, None], runs(n5, H)]) - (np.minimum(h[np.arange(N)[:, None], runs(n4, N)], y))

@@ -1,0 +1,209 @@
+from contextlib import ExitStack
+
+import concourse.mybir as mybir
+
+K, T, S, H, N, W = 512, 2048, 512, 512, 512, 256
+FLOPS = 2 * K * H * S + 2 * H * N * S
+
+F32 = mybir.dt.float32
+BF16 = mybir.dt.bfloat16
+I32 = mybir.dt.int32
+U32 = mybir.dt.uint32
+U16 = mybir.dt.uint16
+U8 = mybir.dt.uint8
+FP8X4 = mybir.dt.float8_e4m3fn_x4
+ALU = mybir.AluOpType
+COPY = mybir.ActivationFunctionType.Copy
+
+P = 128
+PACK = 4
+HALF = 256
+
+
+def deal_views(dealt, raw, half):
+    m = slice(half * P // 2, (half + 1) * P // 2)
+    return (
+        dealt[:, :, m, :].rearrange("p t m j -> p m j t"),
+        raw[:].rearrange("p j (m t) -> p m j t", t=PACK),
+    )
+
+
+def tile_picked_skipmaxbfoldd_none_p_kernel(
+    tc, x_words, x_scales, w1, gn, w2, offs, n1, n2, n3, n4, n5, out
+):
+    nc = tc.nc
+    with ExitStack() as ctx:
+        keep = ctx.enter_context(tc.tile_pool(name="keep", bufs=1))
+        psum = ctx.enter_context(tc.psum_pool(name="psum", bufs=1))
+
+        def new(shape, dtype, name):
+            return keep.tile(shape, dtype, name=name, align_bytes=64)
+
+        l_offs = new([P, S // 16], U16, "l_offs")
+        l_n1 = new([P, W // 16], U16, "l_n1")
+        l_n2 = new([P, W // 16], U16, "l_n2")
+        l_n3 = new([P, S // 16], U16, "l_n3")
+        l_n4 = new([P, S // 16], U16, "l_n4")
+        l_n5 = new([P, S // 16], U16, "l_n5")
+        gain = new([P, PACK], F32, "gain")
+        table_words = new([P, T], U32, "table_words")
+        table_scales = new([P, T], U8, "table_scales")
+        w1_raw = [new([P, PACK, HALF], F32, "w1_raw%d" % h) for h in range(2)]
+        w2_raw = [new([P, PACK, HALF], F32, "w2_raw%d" % h) for h in range(2)]
+
+        nc.vector.memset(table_scales[:].bitcast(I32), 0)
+        scale_rows = new([P, T], U8, "scale_rows")
+        w1_rows = w1.rearrange("(p j) c -> p j c", j=PACK)
+        w2_rows = w2.rearrange("(p j) c -> p j c", j=PACK)
+        nc.sync.dma_start(w1_raw[0][:], w1_rows[:, :, :HALF])
+        for q in range(4):
+            nc.sync.dma_start(
+                scale_rows[32 * q : 32 * q + 4, :].bitcast(I32),
+                x_scales[0][4 * q : 4 * q + 4, :].bitcast(I32),
+            )
+        nc.sync.dma_start(l_offs[:], offs)
+        nc.sync.dma_start(w1_raw[1][:], w1_rows[:, :, HALF:])
+        nc.sync.dma_start(
+            table_words[:].bitcast(I32), x_words[0].rearrange("p n t -> p (n t)").bitcast(I32)
+        )
+        nc.sync.dma_start(gain[:], gn.rearrange("(p t) o -> p (t o)", t=PACK))
+        nc.sync.dma_start(l_n1[:], n1)
+        nc.sync.dma_start(l_n2[:], n2)
+        nc.sync.dma_start(l_n3[:], n3)
+        for h in range(2):
+            nc.sync.dma_start(w2_raw[h][:], w2_rows[:, :, h * HALF : (h + 1) * HALF])
+        nc.sync.dma_start(l_n5[:], n5)
+        nc.sync.dma_start(l_n4[:], n4)
+
+        x_codes = [new([P, HALF], U32, "x_codes%d" % h) for h in range(2)]
+        x_bytes = new([P, S], U8, "x_bytes")
+        for q in range(4):
+            rows = slice(32 * q, 32 * q + 4)
+            nc.vector.tensor_copy(
+                table_scales[rows, :].bitcast(I32), scale_rows[rows, :].bitcast(I32)
+            )
+        nc.vector.tensor_copy(x_bytes[:], table_scales[:].indirect(l_offs[:]))
+
+        w1_dealt = new([P, PACK, P, PACK], BF16, "w1_dealt")
+        for h in range(2):
+            nc.scalar.copy(*deal_views(w1_dealt, w1_raw[h], h))
+        w1_codes = new([P, PACK, P], U32, "w1_codes")
+        w1_bytes = new([P, PACK, P], U8, "w1_bytes")
+        y_bank = [psum.tile([P, S], F32, name="y_bank%d" % t) for t in range(PACK)]
+        h_bank = [psum.tile([P, S], F32, name="h_bank%d" % t) for t in range(PACK)]
+        ds = [new([P, S], F32, "ds%d" % t) for t in range(PACK)]
+        nc.vector.quantize_mx(
+            out=w1_codes[:].rearrange("p t m -> p (t m)").bitcast(FP8X4),
+            scales=w1_bytes[:].rearrange("p t m -> p (t m)"),
+            in_=w1_dealt[:].rearrange("p t m j -> p (t m j)"),
+        )
+        for h in range(2):
+            nc.vector.tensor_copy(
+                x_codes[h][:], table_words[:].indirect(l_offs[:, 16 * h : 16 * (h + 1)])
+            )
+        for t in range(PACK):
+            for h in range(2):
+                cols = slice(h * HALF, (h + 1) * HALF)
+                nc.tensor.matmul_mx(
+                    out=y_bank[t][:, cols],
+                    lhsT=w1_codes[:, t, :].bitcast(FP8X4),
+                    lhsT_scale=w1_bytes[:, t, :],
+                    rhs=x_codes[h][:].bitcast(FP8X4),
+                    rhs_scale=x_bytes[:, cols],
+                    start=True,
+                    stop=True,
+                )
+                if t == 0:
+                    nc.scalar.activation(
+                        ds[t][:, cols], y_bank[t][:, cols], COPY, scale=gain[:, t : t + 1]
+                    )
+            if t > 0:
+                nc.scalar.activation(ds[t][:], y_bank[t][:], COPY, scale=gain[:, t : t + 1])
+
+        pa = [new([P, W], F32, "pa%d" % t) for t in range(PACK)]
+        pb = [new([P, W], F32, "pb%d" % t) for t in range(PACK)]
+        ds_half = [new([P, 2 * S], F32, "ds_half%d" % t) for t in range(PACK)]
+        y_win = [new([P, 2 * S], F32, "y_win%d" % t) for t in range(PACK)]
+        h_win = [new([P, 2 * S], F32, "h_win%d" % t) for t in range(PACK)]
+        z = new([P, PACK, S], F32, "z")
+
+        def fold(t):
+            nc.vector.tensor_tensor(z[:, t, :], ds_half[t][:].indirect(l_n3[:]), ds[t][:], ALU.add)
+
+        for t in range(PACK):
+            nc.vector.tensor_copy(pa[t][:], ds[t][:].indirect(l_n1[:]))
+            nc.vector.tensor_scalar(
+                pb[t][:], ds[t][:].indirect(l_n2[:]), -0.5, 0.0, ALU.mult, ALU.add
+            )
+            if t > 0:
+                fold(t - 1)
+            nc.vector.tensor_tensor(ds[t][:].indirect(l_n2[:]), pa[t][:], pb[t][:], ALU.add)
+            nc.scalar.activation(ds_half[t][:, :S], ds[t][:], COPY, scale=-0.5)
+            nc.scalar.copy(y_win[t][:, :S], y_bank[t][:])
+
+        w2_dealt = new([P, PACK, P, PACK], BF16, "w2_dealt")
+        for h in range(2):
+            nc.scalar.copy(*deal_views(w2_dealt, w2_raw[h], h))
+
+        y_free = new([P, S], F32, "y_free")
+        y_at = [y_free[:], ds[3][:], ds_half[3][:, :S], ds_half[3][:, S:]]
+        nc.vector.tensor_copy(y_at[0], y_win[0][:].indirect(l_n5[:]))
+        fold(PACK - 1)
+
+        w2_codes = new([P, PACK, P], U32, "w2_codes")
+        w2_bytes = new([P, PACK, P], U8, "w2_bytes")
+        nc.vector.quantize_mx(
+            out=w2_codes[:].rearrange("p t m -> p (t m)").bitcast(FP8X4),
+            scales=w2_bytes[:].rearrange("p t m -> p (t m)"),
+            in_=w2_dealt[:].rearrange("p t m j -> p (t m j)"),
+        )
+
+        for h in range(2):
+            cols = slice(h * HALF, (h + 1) * HALF)
+            z_woven = new([P, HALF, PACK], BF16, "z_woven%d" % h)
+            z_codes = new([P, HALF], U32, "z_codes%d" % h)
+            z_bytes = new([P, HALF], U8, "z_bytes%d" % h)
+            nc.scalar.copy(
+                z_woven[:].rearrange("p (c i) t -> p c t i", i=4),
+                z[:, :, cols].rearrange("p t (c i) -> p c t i", i=4),
+            )
+            nc.vector.quantize_mx(
+                out=z_codes[:].bitcast(FP8X4),
+                scales=z_bytes[:],
+                in_=z_woven[:].rearrange("p n t -> p (n t)"),
+            )
+            for t in range(PACK):
+                nc.tensor.matmul_mx(
+                    out=h_bank[t][:, cols],
+                    lhsT=w2_codes[:, t, :].bitcast(FP8X4),
+                    lhsT_scale=w2_bytes[:, t, :],
+                    rhs=z_codes[:].bitcast(FP8X4),
+                    rhs_scale=z_bytes[:],
+                    start=True,
+                    stop=True,
+                )
+        for t in range(1, PACK):
+            nc.vector.tensor_copy(y_at[t], y_win[t][:].indirect(l_n5[:]))
+
+        out_rows = out.rearrange("(p t) n -> p t n", t=PACK)
+        h_at = [new([P, S], F32, "h_at%d" % t) for t in range(PACK)]
+        larger = [new([P, S], F32, "larger%d" % t) for t in range(PACK)]
+        smaller = [new([P, S], F32, "smaller%d" % t) for t in range(PACK)]
+        result = [new([P, S], F32, "result%d" % t) for t in range(PACK)]
+
+        def finish(t, cols):
+            nc.vector.tensor_tensor(
+                result[t][:, cols], larger[t][:, cols], smaller[t][:, cols], ALU.subtract
+            )
+            nc.sync.dma_start(out_rows[:, t, cols], result[t][:, cols])
+
+        for t in range(PACK):
+            nc.scalar.copy(h_win[t][:, :S], h_bank[t][:])
+        for t in range(PACK):
+            nc.vector.tensor_copy(h_at[t][:], h_win[t][:].indirect(l_n4[:]))
+            nc.vector.tensor_tensor(larger[t][:], y_at[t], h_bank[t][:], ALU.max)
+            if t > 0:
+                finish(t - 1, slice(0, S))
+            nc.vector.tensor_tensor(smaller[t][:], h_at[t][:], y_bank[t][:], ALU.min)
+        finish(PACK - 1, slice(0, HALF))
+        finish(PACK - 1, slice(HALF, S))

@@ -127,28 +127,37 @@ def tile_picked_skipmaxbfoldd_none_p_kernel(
         h_win = [new([P, 2 * S], F32, "h_win%d" % t) for t in range(PACK)]
         z = new([P, PACK, S], F32, "z")
 
-        def fold(t):
-            nc.vector.tensor_tensor(z[:, t, :], ds_half[t][:].indirect(l_n3[:]), ds[t][:], ALU.add)
-
+        w2_dealt = new([P, PACK, P, PACK], BF16, "w2_dealt")
+        for h in range(2):
+            nc.scalar.copy(*deal_views(w2_dealt, w2_raw[h], h))
         for t in range(PACK):
+            nc.scalar.copy(y_win[t][:, :S], y_bank[t][:])
+
+        def fetch_pairs(t):
             nc.vector.tensor_copy(pa[t][:], ds[t][:].indirect(l_n1[:]))
             nc.vector.tensor_scalar(
                 pb[t][:], ds[t][:].indirect(l_n2[:]), -0.5, 0.0, ALU.mult, ALU.add
             )
-            if t > 0:
-                fold(t - 1)
+
+        def fold(t, c0, c1):
+            nc.vector.tensor_tensor(
+                z[:, t, c0:c1],
+                ds_half[t][:].indirect(l_n3[:, c0 // 16 : c1 // 16]),
+                ds[t][:, c0:c1],
+                ALU.add,
+            )
+
+        fetch_pairs(0)
+        for t in range(PACK):
+            if t + 1 < PACK:
+                fetch_pairs(t + 1)
             nc.vector.tensor_tensor(ds[t][:].indirect(l_n2[:]), pa[t][:], pb[t][:], ALU.add)
             nc.scalar.activation(ds_half[t][:, :S], ds[t][:], COPY, scale=-0.5)
-            nc.scalar.copy(y_win[t][:, :S], y_bank[t][:])
-
-        w2_dealt = new([P, PACK, P, PACK], BF16, "w2_dealt")
-        for h in range(2):
-            nc.scalar.copy(*deal_views(w2_dealt, w2_raw[h], h))
-
-        y_free = new([P, S], F32, "y_free")
-        y_at = [y_free[:], ds[3][:], ds_half[3][:, :S], ds_half[3][:, S:]]
-        nc.vector.tensor_copy(y_at[0], y_win[0][:].indirect(l_n5[:]))
-        fold(PACK - 1)
+        for t in range(PACK - 1):
+            fold(t, 0, S)
+        fold(PACK - 1, 0, HALF)
+        fold(PACK - 1, HALF, S)
+        y_at = [ds[2][:], ds[3][:], ds_half[3][:, :S], ds_half[3][:, S:]]
 
         w2_codes = new([P, PACK, P], U32, "w2_codes")
         w2_bytes = new([P, PACK, P], U8, "w2_bytes")
@@ -182,7 +191,8 @@ def tile_picked_skipmaxbfoldd_none_p_kernel(
                     start=True,
                     stop=True,
                 )
-        for t in range(1, PACK):
+            nc.scalar.copy(h_win[0][:, cols], h_bank[0][:, cols])
+        for t in range(PACK):
             nc.vector.tensor_copy(y_at[t], y_win[t][:].indirect(l_n5[:]))
 
         out_rows = out.rearrange("(p t) n -> p t n", t=PACK)
@@ -191,19 +201,21 @@ def tile_picked_skipmaxbfoldd_none_p_kernel(
         smaller = [new([P, S], F32, "smaller%d" % t) for t in range(PACK)]
         result = [new([P, S], F32, "result%d" % t) for t in range(PACK)]
 
-        def finish(t, cols):
-            nc.vector.tensor_tensor(
-                result[t][:, cols], larger[t][:, cols], smaller[t][:, cols], ALU.subtract
-            )
-            nc.sync.dma_start(out_rows[:, t, cols], result[t][:, cols])
-
-        for t in range(PACK):
+        for t in range(1, PACK):
             nc.scalar.copy(h_win[t][:, :S], h_bank[t][:])
         for t in range(PACK):
             nc.vector.tensor_copy(h_at[t][:], h_win[t][:].indirect(l_n4[:]))
             nc.vector.tensor_tensor(larger[t][:], y_at[t], h_bank[t][:], ALU.max)
-            if t > 0:
-                finish(t - 1, slice(0, S))
-            nc.vector.tensor_tensor(smaller[t][:], h_at[t][:], y_bank[t][:], ALU.min)
-        finish(PACK - 1, slice(0, HALF))
-        finish(PACK - 1, slice(HALF, S))
+            if t < PACK - 1:
+                nc.vector.tensor_tensor(smaller[t][:], h_at[t][:], y_bank[t][:], ALU.min)
+                nc.gpsimd.tensor_tensor(result[t][:], larger[t][:], smaller[t][:], ALU.subtract)
+                nc.sync.dma_start(out_rows[:, t, :], result[t][:])
+        t = PACK - 1
+        halves = [slice(0, HALF), slice(HALF, S)]
+        for cols in halves:
+            nc.vector.tensor_tensor(smaller[t][:, cols], h_at[t][:, cols], y_bank[t][:, cols], ALU.min)
+        for cols in halves:
+            nc.vector.tensor_tensor(
+                result[t][:, cols], larger[t][:, cols], smaller[t][:, cols], ALU.subtract
+            )
+            nc.sync.dma_start(out_rows[:, t, cols], result[t][:, cols])

@@ -14,6 +14,7 @@ U8 = mybir.dt.uint8
 FP8X4 = mybir.dt.float8_e4m3fn_x4
 ALU = mybir.AluOpType
 COPY = mybir.ActivationFunctionType.Copy
+RELU = mybir.ActivationFunctionType.Relu
 
 P = 128
 PACK = 4
@@ -75,7 +76,7 @@ def tile_picked_skipmaxbfoldd_none_p_kernel(
         nc.sync.dma_start(l_n5[:], n5)
         nc.sync.dma_start(l_n4[:], n4)
 
-        x_codes = [new([P, HALF], U32, "x_codes%d" % h) for h in range(2)]
+        x_codes = new([P, S], U32, "x_codes")
         x_bytes = new([P, S], U8, "x_bytes")
         for q in range(4):
             rows = slice(32 * q, 32 * q + 4)
@@ -97,41 +98,37 @@ def tile_picked_skipmaxbfoldd_none_p_kernel(
             scales=w1_bytes[:].rearrange("p t m -> p (t m)"),
             in_=w1_dealt[:].rearrange("p t m j -> p (t m j)"),
         )
-        for h in range(2):
+        halves = [slice(0, HALF), slice(HALF, S)]
+        for h, cols in enumerate(halves):
             nc.vector.tensor_copy(
-                x_codes[h][:], table_words[:].indirect(l_offs[:, 16 * h : 16 * (h + 1)])
+                x_codes[:, cols], table_words[:].indirect(l_offs[:, 16 * h : 16 * (h + 1)])
             )
-        for t in range(PACK):
-            for h in range(2):
-                cols = slice(h * HALF, (h + 1) * HALF)
-                nc.tensor.matmul_mx(
-                    out=y_bank[t][:, cols],
-                    lhsT=w1_codes[:, t, :].bitcast(FP8X4),
-                    lhsT_scale=w1_bytes[:, t, :],
-                    rhs=x_codes[h][:].bitcast(FP8X4),
-                    rhs_scale=x_bytes[:, cols],
-                    start=True,
-                    stop=True,
-                )
-                if t == 0:
-                    nc.scalar.activation(
-                        ds[t][:, cols], y_bank[t][:, cols], COPY, scale=gain[:, t : t + 1]
-                    )
-            if t > 0:
-                nc.scalar.activation(ds[t][:], y_bank[t][:], COPY, scale=gain[:, t : t + 1])
+        y_parts = [(0, halves[0], y_bank[0]), (0, halves[1], h_bank[PACK - 1])]
+        y_parts = y_parts + [(t, slice(0, S), y_bank[t]) for t in range(1, PACK)]
+        for t, cols, bank in y_parts:
+            nc.tensor.matmul_mx(
+                out=bank[:, cols],
+                lhsT=w1_codes[:, t, :].bitcast(FP8X4),
+                lhsT_scale=w1_bytes[:, t, :],
+                rhs=x_codes[:, cols].bitcast(FP8X4),
+                rhs_scale=x_bytes[:, cols],
+                start=True,
+                stop=True,
+            )
+            nc.scalar.activation(ds[t][:, cols], bank[:, cols], COPY, scale=gain[:, t : t + 1])
 
         pa = [new([P, W], F32, "pa%d" % t) for t in range(PACK)]
         pb = [new([P, W], F32, "pb%d" % t) for t in range(PACK)]
         ds_half = [new([P, 2 * S], F32, "ds_half%d" % t) for t in range(PACK)]
         y_win = [new([P, 2 * S], F32, "y_win%d" % t) for t in range(PACK)]
-        h_win = [new([P, 2 * S], F32, "h_win%d" % t) for t in range(PACK)]
+        h_win = [new([P, 2 * S if t < PACK - 1 else S], F32, "h_win%d" % t) for t in range(PACK)]
         z = new([P, PACK, S], F32, "z")
 
         w2_dealt = new([P, PACK, P, PACK], BF16, "w2_dealt")
         for h in range(2):
             nc.scalar.copy(*deal_views(w2_dealt, w2_raw[h], h))
-        for t in range(PACK):
-            nc.scalar.copy(y_win[t][:, :S], y_bank[t][:])
+        for t, cols, bank in y_parts:
+            nc.scalar.copy(y_win[t][:, cols], bank[:, cols])
 
         def fetch_pairs(t):
             nc.vector.tensor_copy(pa[t][:], ds[t][:].indirect(l_n1[:]))
@@ -157,7 +154,6 @@ def tile_picked_skipmaxbfoldd_none_p_kernel(
             fold(t, 0, S)
         fold(PACK - 1, 0, HALF)
         fold(PACK - 1, HALF, S)
-        y_at = [ds[2][:], ds[3][:], ds_half[3][:, :S], ds_half[3][:, S:]]
 
         w2_codes = new([P, PACK, P], U32, "w2_codes")
         w2_bytes = new([P, PACK, P], U8, "w2_bytes")
@@ -191,7 +187,9 @@ def tile_picked_skipmaxbfoldd_none_p_kernel(
                     start=True,
                     stop=True,
                 )
-            nc.scalar.copy(h_win[0][:, cols], h_bank[0][:, cols])
+            nc.scalar.activation(h_win[0][:, cols], h_bank[0][:, cols], COPY, scale=-1.0)
+        y_after_half = new([P, S], F32, "z_woven0")
+        y_at = [ds[3][:], y_after_half[:], z[:, 0, :], z[:, 1, :]]
         for t in range(PACK):
             nc.vector.tensor_copy(y_at[t], y_win[t][:].indirect(l_n5[:]))
 
@@ -203,19 +201,46 @@ def tile_picked_skipmaxbfoldd_none_p_kernel(
 
         for t in range(1, PACK):
             nc.scalar.copy(h_win[t][:, :S], h_bank[t][:])
-        for t in range(PACK):
+
+        y0 = y_win[0][:, :S]
+        nc.vector.tensor_tensor(h_at[0][:], h_win[0][:].indirect(l_n4[:]), y0, ALU.add)
+        nc.vector.tensor_tensor(larger[0][:], y_at[0], h_bank[0][:], ALU.max)
+        nc.scalar.activation(smaller[0][:], h_at[0][:], RELU)
+        above_y = new([P, S], F32, "above_y")
+        nc.gpsimd.tensor_tensor(above_y[:], larger[0][:], y0, ALU.subtract)
+        nc.gpsimd.tensor_tensor(result[0][:], above_y[:], smaller[0][:], ALU.add)
+        nc.sync.dma_start(out_rows[:, 0, :], result[0][:])
+        for t in range(1, PACK - 1):
             nc.vector.tensor_copy(h_at[t][:], h_win[t][:].indirect(l_n4[:]))
             nc.vector.tensor_tensor(larger[t][:], y_at[t], h_bank[t][:], ALU.max)
-            if t < PACK - 1:
-                nc.vector.tensor_tensor(smaller[t][:], h_at[t][:], y_bank[t][:], ALU.min)
-                nc.gpsimd.tensor_tensor(result[t][:], larger[t][:], smaller[t][:], ALU.subtract)
-                nc.sync.dma_start(out_rows[:, t, :], result[t][:])
+            nc.vector.tensor_tensor(smaller[t][:], h_at[t][:], y_bank[t][:], ALU.min)
+            nc.gpsimd.tensor_tensor(result[t][:], larger[t][:], smaller[t][:], ALU.subtract)
+            nc.sync.dma_start(out_rows[:, t, :], result[t][:])
+
         t = PACK - 1
-        halves = [slice(0, HALF), slice(HALF, S)]
-        for cols in halves:
+        pieces = [slice(0, 256), slice(256, 384), slice(384, 512)]
+
+        def fetch(cols):
+            nc.vector.tensor_copy(
+                h_at[t][:, cols], h_win[t][:].indirect(l_n4[:, cols.start // 16 : cols.stop // 16])
+            )
+
+        def least(cols):
             nc.vector.tensor_tensor(smaller[t][:, cols], h_at[t][:, cols], y_bank[t][:, cols], ALU.min)
-        for cols in halves:
-            nc.vector.tensor_tensor(
+
+        def finish(engine, cols):
+            engine.tensor_tensor(
                 result[t][:, cols], larger[t][:, cols], smaller[t][:, cols], ALU.subtract
             )
             nc.sync.dma_start(out_rows[:, t, cols], result[t][:, cols])
+
+        fetch(pieces[0])
+        nc.vector.tensor_tensor(larger[t][:], y_at[t], h_bank[t][:], ALU.max)
+        least(pieces[0])
+        finish(nc.gpsimd, pieces[0])
+        fetch(pieces[1])
+        fetch(pieces[2])
+        least(pieces[1])
+        least(pieces[2])
+        finish(nc.vector, pieces[1])
+        finish(nc.vector, pieces[2])

@@ -1,6 +1,7 @@
 from contextlib import ExitStack
 
 import concourse.mybir as mybir
+from concourse.masks import make_identity
 
 K, T, S, H, N, W = 512, 2048, 512, 512, 512, 256
 FLOPS = 2 * K * H * S + 2 * H * N * S
@@ -19,6 +20,7 @@ RELU = mybir.ActivationFunctionType.Relu
 P = 128
 PACK = 4
 HALF = 256
+SUMMED = 2
 
 
 def deal_views(dealt, raw, half):
@@ -119,16 +121,38 @@ def tile_picked_skipmaxbfoldd_none_p_kernel(
 
         pa = [new([P, W], F32, "pa%d" % t) for t in range(PACK)]
         pb = [new([P, W], F32, "pb%d" % t) for t in range(PACK)]
-        ds_half = [new([P, 2 * S], F32, "ds_half%d" % t) for t in range(PACK)]
+        ds_half = [new([P, S], F32, "ds_half%d" % t) for t in range(PACK)]
         y_win = [new([P, 2 * S], F32, "y_win%d" % t) for t in range(PACK)]
-        h_win = [new([P, 2 * S if t < PACK - 1 else S], F32, "h_win%d" % t) for t in range(PACK)]
-        z = new([P, PACK, S], F32, "z")
+        h_win = [new([P, 2 * S], F32, "h_win%d" % t) for t in range(PACK)]
+        minus_half = new([P, 1], F32, "z1")
+        nc.gpsimd.memset(minus_half[:], -0.5)
 
         w2_dealt = new([P, PACK, P, PACK], BF16, "w2_dealt")
         for h in range(2):
             nc.scalar.copy(*deal_views(w2_dealt, w2_raw[h], h))
         for t, cols, bank in y_parts:
-            nc.scalar.copy(y_win[t][:, cols], bank[:, cols])
+            nc.scalar.activation(
+                y_win[t][:, cols], bank[:, cols], COPY, scale=-1.0 if t < SUMMED else 1.0
+            )
+
+        identity = new([P, P], F32, "identity")
+        make_identity(nc, identity[:])
+
+        def add_turned(bank, term, first, last):
+            for c in range(PACK):
+                block = slice(c * P, (c + 1) * P)
+                nc.tensor.matmul(
+                    bank[:, block],
+                    lhsT=term[:, block],
+                    rhs=identity[:],
+                    is_transpose=True,
+                    start=first and c == 0,
+                    stop=last and c == PACK - 1,
+                )
+
+        sum_bank = [psum.tile([P, S], F32, name="y_bank%d" % t) for t in range(SUMMED)]
+        for t in range(SUMMED):
+            add_turned(sum_bank[t], y_win[t][:, :S], True, False)
 
         def fetch_pairs(t):
             nc.vector.tensor_copy(pa[t][:], ds[t][:].indirect(l_n1[:]))
@@ -136,24 +160,22 @@ def tile_picked_skipmaxbfoldd_none_p_kernel(
                 pb[t][:], ds[t][:].indirect(l_n2[:]), -0.5, 0.0, ALU.mult, ALU.add
             )
 
-        def fold(t, c0, c1):
-            nc.vector.tensor_tensor(
-                z[:, t, c0:c1],
-                ds_half[t][:].indirect(l_n3[:, c0 // 16 : c1 // 16]),
-                ds[t][:, c0:c1],
-                ALU.add,
-            )
 
         fetch_pairs(0)
         for t in range(PACK):
             if t + 1 < PACK:
                 fetch_pairs(t + 1)
             nc.vector.tensor_tensor(ds[t][:].indirect(l_n2[:]), pa[t][:], pb[t][:], ALU.add)
-            nc.scalar.activation(ds_half[t][:, :S], ds[t][:], COPY, scale=-0.5)
-        for t in range(PACK - 1):
-            fold(t, 0, S)
-        fold(PACK - 1, 0, HALF)
-        fold(PACK - 1, HALF, S)
+            nc.scalar.activation(ds_half[t][:, :S], ds[t][:], COPY, scale=minus_half[:])
+        z = [new([P, PACK, HALF], F32, "z%d" % h) for h in range(2)]
+        for h, cols in enumerate(halves):
+            for t in range(PACK):
+                nc.vector.tensor_tensor(
+                    z[h][:, t, :],
+                    ds_half[t][:].indirect(l_n3[:, 16 * h : 16 * (h + 1)]),
+                    ds[t][:, cols],
+                    ALU.add,
+                )
 
         w2_codes = new([P, PACK, P], U32, "w2_codes")
         w2_bytes = new([P, PACK, P], U8, "w2_bytes")
@@ -170,7 +192,7 @@ def tile_picked_skipmaxbfoldd_none_p_kernel(
             z_bytes = new([P, HALF], U8, "z_bytes%d" % h)
             nc.scalar.copy(
                 z_woven[:].rearrange("p (c i) t -> p c t i", i=4),
-                z[:, :, cols].rearrange("p t (c i) -> p c t i", i=4),
+                z[h][:].rearrange("p t (c i) -> p c t i", i=4),
             )
             nc.vector.quantize_mx(
                 out=z_codes[:].bitcast(FP8X4),
@@ -187,30 +209,42 @@ def tile_picked_skipmaxbfoldd_none_p_kernel(
                     start=True,
                     stop=True,
                 )
-            nc.scalar.activation(h_win[0][:, cols], h_bank[0][:, cols], COPY, scale=-1.0)
-        y_after_half = new([P, S], F32, "z_woven0")
-        y_at = [ds[3][:], y_after_half[:], z[:, 0, :], z[:, 1, :]]
-        for t in range(PACK):
+            nc.scalar.copy(h_win[0][:, cols], h_bank[0][:, cols])
+        y_at = {SUMMED + h: new([P, S], F32, "z_woven%d" % h)[:] for h in range(2)}
+        for t in range(SUMMED, PACK):
             nc.vector.tensor_copy(y_at[t], y_win[t][:].indirect(l_n5[:]))
 
         out_rows = out.rearrange("(p t) n -> p t n", t=PACK)
         h_at = [new([P, S], F32, "h_at%d" % t) for t in range(PACK)]
         larger = [new([P, S], F32, "larger%d" % t) for t in range(PACK)]
         smaller = [new([P, S], F32, "smaller%d" % t) for t in range(PACK)]
-        result = [new([P, S], F32, "result%d" % t) for t in range(PACK)]
+        result = [new([P, S], F32, "result%d" % t) for t in range(PACK - 1)] + [larger[PACK - 2]]
 
         for t in range(1, PACK):
             nc.scalar.copy(h_win[t][:, :S], h_bank[t][:])
 
-        y0 = y_win[0][:, :S]
-        nc.vector.tensor_tensor(h_at[0][:], h_win[0][:].indirect(l_n4[:]), y0, ALU.add)
-        nc.vector.tensor_tensor(larger[0][:], y_at[0], h_bank[0][:], ALU.max)
-        nc.scalar.activation(smaller[0][:], h_at[0][:], RELU)
-        above_y = new([P, S], F32, "above_y")
-        nc.gpsimd.tensor_tensor(above_y[:], larger[0][:], y0, ALU.subtract)
-        nc.gpsimd.tensor_tensor(result[0][:], above_y[:], smaller[0][:], ALU.add)
-        nc.sync.dma_start(out_rows[:, 0, :], result[0][:])
-        for t in range(1, PACK - 1):
+        for t in range(SUMMED):
+            h_t = h_win[t][:, :S]
+            add_turned(sum_bank[t], h_t, False, False)
+            gap_max = new([P, S], F32, "gap_max%d" % t)
+            nc.vector.tensor_tensor(gap_max[:], y_win[t][:].indirect(l_n5[:]), h_t, ALU.add)
+            nc.scalar.activation(larger[t][:], gap_max[:], RELU, scale=-1.0)
+            add_turned(sum_bank[t], larger[t], False, False)
+            nc.vector.tensor_tensor(
+                h_at[t][:], h_win[t][:].indirect(l_n4[:]), y_win[t][:, :S], ALU.add
+            )
+            nc.scalar.activation(smaller[t][:], h_at[t][:], RELU, scale=-1.0)
+            add_turned(sum_bank[t], smaller[t], False, True)
+        for t in range(SUMMED):
+            turned = new([P, S], F32, "turned%d" % t)
+            nc.scalar.copy(turned[:], sum_bank[t][:])
+            back_bank = psum.tile([P, S], F32, name="h_bank%d" % t)
+            for c in range(PACK):
+                block = slice(c * P, (c + 1) * P)
+                nc.tensor.transpose(back_bank[:, block], turned[:, block], identity[:])
+            nc.scalar.copy(result[t][:], back_bank[:])
+            nc.scalar.dma_start(out_rows[:, t, :], result[t][:])
+        for t in range(SUMMED, PACK - 1):
             nc.vector.tensor_copy(h_at[t][:], h_win[t][:].indirect(l_n4[:]))
             nc.vector.tensor_tensor(larger[t][:], y_at[t], h_bank[t][:], ALU.max)
             nc.vector.tensor_tensor(smaller[t][:], h_at[t][:], y_bank[t][:], ALU.min)
@@ -218,29 +252,12 @@ def tile_picked_skipmaxbfoldd_none_p_kernel(
             nc.sync.dma_start(out_rows[:, t, :], result[t][:])
 
         t = PACK - 1
-        pieces = [slice(0, 256), slice(256, 384), slice(384, 512)]
-
-        def fetch(cols):
-            nc.vector.tensor_copy(
-                h_at[t][:, cols], h_win[t][:].indirect(l_n4[:, cols.start // 16 : cols.stop // 16])
-            )
-
-        def least(cols):
+        nc.vector.tensor_copy(h_at[t][:], h_win[t][:].indirect(l_n4[:]))
+        nc.vector.tensor_tensor(larger[t][:], y_at[t], h_bank[t][:], ALU.max)
+        for cols in halves:
             nc.vector.tensor_tensor(smaller[t][:, cols], h_at[t][:, cols], y_bank[t][:, cols], ALU.min)
-
-        def finish(engine, cols):
-            engine.tensor_tensor(
+        for cols in halves:
+            nc.vector.tensor_tensor(
                 result[t][:, cols], larger[t][:, cols], smaller[t][:, cols], ALU.subtract
             )
             nc.sync.dma_start(out_rows[:, t, cols], result[t][:, cols])
-
-        fetch(pieces[0])
-        nc.vector.tensor_tensor(larger[t][:], y_at[t], h_bank[t][:], ALU.max)
-        least(pieces[0])
-        finish(nc.gpsimd, pieces[0])
-        fetch(pieces[1])
-        fetch(pieces[2])
-        least(pieces[1])
-        least(pieces[2])
-        finish(nc.vector, pieces[1])
-        finish(nc.vector, pieces[2])

@@ -19,8 +19,14 @@ RELU = mybir.ActivationFunctionType.Relu
 
 P = 128
 PACK = 4
+QUADRANTS = 4
+GROUP = 16
 HALF = 256
-SUMMED = 2
+LAST = PACK - 1
+
+
+def entries(cols):
+    return slice(cols.start // GROUP, cols.stop // GROUP)
 
 
 def deal_views(dealt, raw, half):
@@ -35,19 +41,38 @@ def tile_picked_skipmaxbfoldd_none_p_kernel(
     tc, x_words, x_scales, w1, gn, w2, offs, n1, n2, n3, n4, n5, out
 ):
     nc = tc.nc
+    halves = [slice(0, HALF), slice(HALF, 2 * HALF)]
     with ExitStack() as ctx:
         keep = ctx.enter_context(tc.tile_pool(name="keep", bufs=1))
         psum = ctx.enter_context(tc.psum_pool(name="psum", bufs=1))
 
-        def new(shape, dtype, name):
-            return keep.tile(shape, dtype, name=name, align_bytes=64)
+        def new(shape, dtype, name, tag=""):
+            return keep.tile(shape, dtype, name=name, tag=tag or name, align_bytes=64)
 
-        l_offs = new([P, S // 16], U16, "l_offs")
-        l_n1 = new([P, W // 16], U16, "l_n1")
-        l_n2 = new([P, W // 16], U16, "l_n2")
-        l_n3 = new([P, S // 16], U16, "l_n3")
-        l_n4 = new([P, S // 16], U16, "l_n4")
-        l_n5 = new([P, S // 16], U16, "l_n5")
+        def quantize_weight(dealt, codes, scales):
+            nc.vector.quantize_mx(
+                out=codes[:].rearrange("p t m -> p (t m)").bitcast(FP8X4),
+                scales=scales[:].rearrange("p t m -> p (t m)"),
+                in_=dealt[:].rearrange("p t m j -> p (t m j)"),
+            )
+
+        def product(result, w_codes, w_scales, codes, scales):
+            nc.tensor.matmul_mx(
+                out=result,
+                lhsT=w_codes.bitcast(FP8X4),
+                lhsT_scale=w_scales,
+                rhs=codes.bitcast(FP8X4),
+                rhs_scale=scales,
+                start=True,
+                stop=True,
+            )
+
+        l_offs = new([P, S // GROUP], U16, "l_offs")
+        l_n1 = new([P, W // GROUP], U16, "l_n1")
+        l_n2 = new([P, W // GROUP], U16, "l_n2")
+        l_n3 = new([P, S // GROUP], U16, "l_n3")
+        l_n4 = new([P, S // GROUP], U16, "l_n4")
+        l_n5 = new([P, S // GROUP], U16, "l_n5")
         gain = new([P, PACK], F32, "gain")
         table_words = new([P, T], U32, "table_words")
         table_scales = new([P, T], U8, "table_scales")
@@ -56,32 +81,31 @@ def tile_picked_skipmaxbfoldd_none_p_kernel(
 
         nc.vector.memset(table_scales[:].bitcast(I32), 0)
         scale_rows = new([P, T], U8, "scale_rows")
+        live_rows = [slice(32 * q, 32 * q + 4) for q in range(QUADRANTS)]
         w1_rows = w1.rearrange("(p j) c -> p j c", j=PACK)
         w2_rows = w2.rearrange("(p j) c -> p j c", j=PACK)
-        nc.sync.dma_start(w1_raw[0][:], w1_rows[:, :, :HALF])
-        for q in range(4):
+        nc.sync.dma_start(w1_raw[0][:], w1_rows[:, :, halves[0]])
+        for q, rows in enumerate(live_rows):
             nc.sync.dma_start(
-                scale_rows[32 * q : 32 * q + 4, :].bitcast(I32),
-                x_scales[0][4 * q : 4 * q + 4, :].bitcast(I32),
+                scale_rows[rows, :].bitcast(I32), x_scales[0][4 * q : 4 * q + 4, :].bitcast(I32)
             )
         nc.sync.dma_start(l_offs[:], offs)
-        nc.sync.dma_start(w1_raw[1][:], w1_rows[:, :, HALF:])
+        nc.sync.dma_start(w1_raw[1][:], w1_rows[:, :, halves[1]])
         nc.sync.dma_start(
-            table_words[:].bitcast(I32), x_words[0].rearrange("p n t -> p (n t)").bitcast(I32)
+            table_words[:].bitcast(I32), x_words[0].rearrange("p n j -> p (n j)").bitcast(I32)
         )
         nc.sync.dma_start(gain[:], gn.rearrange("(p t) o -> p (t o)", t=PACK))
         nc.sync.dma_start(l_n1[:], n1)
         nc.sync.dma_start(l_n2[:], n2)
         nc.sync.dma_start(l_n3[:], n3)
-        for h in range(2):
-            nc.sync.dma_start(w2_raw[h][:], w2_rows[:, :, h * HALF : (h + 1) * HALF])
+        for h, cols in enumerate(halves):
+            nc.sync.dma_start(w2_raw[h][:], w2_rows[:, :, cols])
         nc.sync.dma_start(l_n5[:], n5)
         nc.sync.dma_start(l_n4[:], n4)
 
         x_codes = new([P, S], U32, "x_codes")
         x_bytes = new([P, S], U8, "x_bytes")
-        for q in range(4):
-            rows = slice(32 * q, 32 * q + 4)
+        for rows in live_rows:
             nc.vector.tensor_copy(
                 table_scales[rows, :].bitcast(I32), scale_rows[rows, :].bitcast(I32)
             )
@@ -95,36 +119,25 @@ def tile_picked_skipmaxbfoldd_none_p_kernel(
         y_bank = [psum.tile([P, S], F32, name="y_bank%d" % t) for t in range(PACK)]
         h_bank = [psum.tile([P, S], F32, name="h_bank%d" % t) for t in range(PACK)]
         ds = [new([P, S], F32, "ds%d" % t) for t in range(PACK)]
-        nc.vector.quantize_mx(
-            out=w1_codes[:].rearrange("p t m -> p (t m)").bitcast(FP8X4),
-            scales=w1_bytes[:].rearrange("p t m -> p (t m)"),
-            in_=w1_dealt[:].rearrange("p t m j -> p (t m j)"),
-        )
-        halves = [slice(0, HALF), slice(HALF, S)]
-        for h, cols in enumerate(halves):
+        quantize_weight(w1_dealt, w1_codes, w1_bytes)
+        for cols in halves:
             nc.vector.tensor_copy(
-                x_codes[:, cols], table_words[:].indirect(l_offs[:, 16 * h : 16 * (h + 1)])
+                x_codes[:, cols], table_words[:].indirect(l_offs[:, entries(cols)])
             )
-        y_parts = [(0, halves[0], y_bank[0]), (0, halves[1], h_bank[PACK - 1])]
+        y_parts = [(0, halves[0], y_bank[0]), (0, halves[1], h_bank[LAST])]
         y_parts = y_parts + [(t, slice(0, S), y_bank[t]) for t in range(1, PACK)]
         for t, cols, bank in y_parts:
-            nc.tensor.matmul_mx(
-                out=bank[:, cols],
-                lhsT=w1_codes[:, t, :].bitcast(FP8X4),
-                lhsT_scale=w1_bytes[:, t, :],
-                rhs=x_codes[:, cols].bitcast(FP8X4),
-                rhs_scale=x_bytes[:, cols],
-                start=True,
-                stop=True,
+            product(
+                bank[:, cols], w1_codes[:, t, :], w1_bytes[:, t, :], x_codes[:, cols], x_bytes[:, cols]
             )
             nc.scalar.activation(ds[t][:, cols], bank[:, cols], COPY, scale=gain[:, t : t + 1])
 
         pa = [new([P, W], F32, "pa%d" % t) for t in range(PACK)]
-        pb = [new([P, W], F32, "pb%d" % t) for t in range(PACK)]
+        pb_half = [new([P, W], F32, "pb_half%d" % t) for t in range(PACK)]
         ds_half = [new([P, S], F32, "ds_half%d" % t) for t in range(PACK)]
         y_win = [new([P, 2 * S], F32, "y_win%d" % t) for t in range(PACK)]
         h_win = [new([P, 2 * S], F32, "h_win%d" % t) for t in range(PACK)]
-        minus_half = new([P, 1], F32, "z1")
+        minus_half = new([P, 1], F32, "minus_half", tag="z1")
         nc.gpsimd.memset(minus_half[:], -0.5)
 
         w2_dealt = new([P, PACK, P, PACK], BF16, "w2_dealt")
@@ -132,61 +145,55 @@ def tile_picked_skipmaxbfoldd_none_p_kernel(
             nc.scalar.copy(*deal_views(w2_dealt, w2_raw[h], h))
         for t, cols, bank in y_parts:
             nc.scalar.activation(
-                y_win[t][:, cols], bank[:, cols], COPY, scale=-1.0 if t < SUMMED else 1.0
+                y_win[t][:, cols], bank[:, cols], COPY, scale=-1.0 if t == 0 else 1.0
             )
 
         identity = new([P, P], F32, "identity")
         make_identity(nc, identity[:])
+        blocks = [slice(c * P, (c + 1) * P) for c in range(S // P)]
+        sum_bank = psum.tile([P, S], F32, name="sum_bank", tag="y_bank0")
 
-        def add_turned(bank, term, first, last):
-            for c in range(PACK):
-                block = slice(c * P, (c + 1) * P)
+        def add_turned(term, first=False, last=False):
+            for block in blocks:
                 nc.tensor.matmul(
-                    bank[:, block],
+                    sum_bank[:, block],
                     lhsT=term[:, block],
                     rhs=identity[:],
                     is_transpose=True,
-                    start=first and c == 0,
-                    stop=last and c == PACK - 1,
+                    start=first and block == blocks[0],
+                    stop=last and block == blocks[-1],
                 )
 
-        sum_bank = [psum.tile([P, S], F32, name="y_bank%d" % t) for t in range(SUMMED)]
-        for t in range(SUMMED):
-            add_turned(sum_bank[t], y_win[t][:, :S], True, False)
+        minus_y0 = y_win[0][:, :S]
+        add_turned(minus_y0, first=True)
 
         def fetch_pairs(t):
             nc.vector.tensor_copy(pa[t][:], ds[t][:].indirect(l_n1[:]))
             nc.vector.tensor_scalar(
-                pb[t][:], ds[t][:].indirect(l_n2[:]), -0.5, 0.0, ALU.mult, ALU.add
+                pb_half[t][:], ds[t][:].indirect(l_n2[:]), -0.5, 0.0, ALU.mult, ALU.add
             )
-
 
         fetch_pairs(0)
         for t in range(PACK):
-            if t + 1 < PACK:
+            if t < LAST:
                 fetch_pairs(t + 1)
-            nc.vector.tensor_tensor(ds[t][:].indirect(l_n2[:]), pa[t][:], pb[t][:], ALU.add)
-            nc.scalar.activation(ds_half[t][:, :S], ds[t][:], COPY, scale=minus_half[:])
+            nc.vector.tensor_tensor(ds[t][:].indirect(l_n2[:]), pa[t][:], pb_half[t][:], ALU.add)
+            nc.scalar.activation(ds_half[t][:], ds[t][:], COPY, scale=minus_half[:])
+
         z = [new([P, PACK, HALF], F32, "z%d" % h) for h in range(2)]
         for h, cols in enumerate(halves):
             for t in range(PACK):
                 nc.vector.tensor_tensor(
                     z[h][:, t, :],
-                    ds_half[t][:].indirect(l_n3[:, 16 * h : 16 * (h + 1)]),
+                    ds_half[t][:].indirect(l_n3[:, entries(cols)]),
                     ds[t][:, cols],
                     ALU.add,
                 )
 
         w2_codes = new([P, PACK, P], U32, "w2_codes")
         w2_bytes = new([P, PACK, P], U8, "w2_bytes")
-        nc.vector.quantize_mx(
-            out=w2_codes[:].rearrange("p t m -> p (t m)").bitcast(FP8X4),
-            scales=w2_bytes[:].rearrange("p t m -> p (t m)"),
-            in_=w2_dealt[:].rearrange("p t m j -> p (t m j)"),
-        )
-
-        for h in range(2):
-            cols = slice(h * HALF, (h + 1) * HALF)
+        quantize_weight(w2_dealt, w2_codes, w2_bytes)
+        for h, cols in enumerate(halves):
             z_woven = new([P, HALF, PACK], BF16, "z_woven%d" % h)
             z_codes = new([P, HALF], U32, "z_codes%d" % h)
             z_bytes = new([P, HALF], U8, "z_bytes%d" % h)
@@ -200,64 +207,67 @@ def tile_picked_skipmaxbfoldd_none_p_kernel(
                 in_=z_woven[:].rearrange("p n t -> p (n t)"),
             )
             for t in range(PACK):
-                nc.tensor.matmul_mx(
-                    out=h_bank[t][:, cols],
-                    lhsT=w2_codes[:, t, :].bitcast(FP8X4),
-                    lhsT_scale=w2_bytes[:, t, :],
-                    rhs=z_codes[:].bitcast(FP8X4),
-                    rhs_scale=z_bytes[:],
-                    start=True,
-                    stop=True,
+                product(
+                    h_bank[t][:, cols], w2_codes[:, t, :], w2_bytes[:, t, :], z_codes[:], z_bytes[:]
                 )
             nc.scalar.copy(h_win[0][:, cols], h_bank[0][:, cols])
-        y_at = {SUMMED + h: new([P, S], F32, "z_woven%d" % h)[:] for h in range(2)}
-        for t in range(SUMMED, PACK):
-            nc.vector.tensor_copy(y_at[t], y_win[t][:].indirect(l_n5[:]))
+
+        y5_first = new([P, S], F32, "y5_first", tag="z_woven0")
+        y5_rest = new([P, 2, S], F32, "y5_rest", tag="z_woven1")
+        y5 = {1: y5_first[:], 2: y5_rest[:, 0, :], 3: y5_rest[:, 1, :]}
+        for t in range(1, PACK):
+            nc.vector.tensor_copy(y5[t], y_win[t][:].indirect(l_n5[:]))
 
         out_rows = out.rearrange("(p t) n -> p t n", t=PACK)
-        h_at = [new([P, S], F32, "h_at%d" % t) for t in range(PACK)]
-        larger = [new([P, S], F32, "larger%d" % t) for t in range(PACK)]
-        smaller = [new([P, S], F32, "smaller%d" % t) for t in range(PACK)]
-        result = [new([P, S], F32, "result%d" % t) for t in range(PACK - 1)] + [larger[PACK - 2]]
+        from_n4 = [new([P, S], F32, "from_n4_%d" % t) for t in range(PACK)]
+        upper = [new([P, S], F32, "upper%d" % t) for t in range(PACK)]
+        lower = [new([P, S], F32, "lower%d" % t) for t in range(PACK)]
+        result = [new([P, S], F32, "result%d" % t) for t in range(LAST)] + [upper[2]]
 
         for t in range(1, PACK):
             nc.scalar.copy(h_win[t][:, :S], h_bank[t][:])
 
-        for t in range(SUMMED):
-            h_t = h_win[t][:, :S]
-            add_turned(sum_bank[t], h_t, False, False)
-            gap_max = new([P, S], F32, "gap_max%d" % t)
-            nc.vector.tensor_tensor(gap_max[:], y_win[t][:].indirect(l_n5[:]), h_t, ALU.add)
-            nc.scalar.activation(larger[t][:], gap_max[:], RELU, scale=-1.0)
-            add_turned(sum_bank[t], larger[t], False, False)
-            nc.vector.tensor_tensor(
-                h_at[t][:], h_win[t][:].indirect(l_n4[:]), y_win[t][:, :S], ALU.add
-            )
-            nc.scalar.activation(smaller[t][:], h_at[t][:], RELU, scale=-1.0)
-            add_turned(sum_bank[t], smaller[t], False, True)
-        for t in range(SUMMED):
-            turned = new([P, S], F32, "turned%d" % t)
-            nc.scalar.copy(turned[:], sum_bank[t][:])
-            back_bank = psum.tile([P, S], F32, name="h_bank%d" % t)
-            for c in range(PACK):
-                block = slice(c * P, (c + 1) * P)
-                nc.tensor.transpose(back_bank[:, block], turned[:, block], identity[:])
-            nc.scalar.copy(result[t][:], back_bank[:])
-            nc.scalar.dma_start(out_rows[:, t, :], result[t][:])
-        for t in range(SUMMED, PACK - 1):
-            nc.vector.tensor_copy(h_at[t][:], h_win[t][:].indirect(l_n4[:]))
-            nc.vector.tensor_tensor(larger[t][:], y_at[t], h_bank[t][:], ALU.max)
-            nc.vector.tensor_tensor(smaller[t][:], h_at[t][:], y_bank[t][:], ALU.min)
-            nc.gpsimd.tensor_tensor(result[t][:], larger[t][:], smaller[t][:], ALU.subtract)
-            nc.sync.dma_start(out_rows[:, t, :], result[t][:])
+        h0 = h_win[0][:, :S]
+        add_turned(h0)
+        h_less_y5 = new([P, S], F32, "h_less_y5")
+        nc.vector.tensor_tensor(h_less_y5[:], y_win[0][:].indirect(l_n5[:]), h0, ALU.add)
+        nc.scalar.activation(upper[0][:], h_less_y5[:], RELU, scale=-1.0)
+        add_turned(upper[0])
+        nc.vector.tensor_tensor(from_n4[0][:], h_win[0][:].indirect(l_n4[:]), minus_y0, ALU.add)
+        nc.scalar.activation(lower[0][:], from_n4[0][:], RELU, scale=-1.0)
+        add_turned(lower[0], last=True)
 
-        t = PACK - 1
-        nc.vector.tensor_copy(h_at[t][:], h_win[t][:].indirect(l_n4[:]))
-        nc.vector.tensor_tensor(larger[t][:], y_at[t], h_bank[t][:], ALU.max)
-        for cols in halves:
-            nc.vector.tensor_tensor(smaller[t][:, cols], h_at[t][:, cols], y_bank[t][:, cols], ALU.min)
+        y1 = y_win[1][:, :S]
+        nc.vector.tensor_tensor(from_n4[1][:], h_win[1][:].indirect(l_n4[:]), y1, ALU.subtract)
+        nc.vector.tensor_tensor(upper[1][:], y5[1], h_bank[1][:], ALU.max)
+        nc.scalar.activation(lower[1][:], from_n4[1][:], RELU, scale=-1.0)
+        upper_less_y = new([P, S], F32, "upper_less_y")
+        nc.gpsimd.tensor_tensor(upper_less_y[:], upper[1][:], y1, ALU.subtract)
+        nc.gpsimd.tensor_tensor(result[1][:], upper_less_y[:], lower[1][:], ALU.add)
+        nc.sync.dma_start(out_rows[:, 1, :], result[1][:])
+
+        turned = new([P, S], F32, "turned")
+        nc.scalar.copy(turned[:], sum_bank[:])
+        back_bank = psum.tile([P, S], F32, name="back_bank", tag="h_bank0")
+        for block in blocks:
+            nc.tensor.transpose(back_bank[:, block], turned[:, block], identity[:])
+        nc.scalar.copy(result[0][:], back_bank[:])
+        nc.scalar.dma_start(out_rows[:, 0, :], result[0][:])
+
+        nc.vector.tensor_copy(from_n4[2][:], h_win[2][:].indirect(l_n4[:]))
+        nc.vector.tensor_tensor(upper[2][:], y5[2], h_bank[2][:], ALU.max)
+        nc.vector.tensor_tensor(lower[2][:], from_n4[2][:], y_bank[2][:], ALU.min)
+        nc.gpsimd.tensor_tensor(result[2][:], upper[2][:], lower[2][:], ALU.subtract)
+        nc.sync.dma_start(out_rows[:, 2, :], result[2][:])
+
+        nc.vector.tensor_copy(from_n4[3][:], h_win[3][:].indirect(l_n4[:]))
+        nc.vector.tensor_tensor(upper[3][:], y5[3], h_bank[3][:], ALU.max)
         for cols in halves:
             nc.vector.tensor_tensor(
-                result[t][:, cols], larger[t][:, cols], smaller[t][:, cols], ALU.subtract
+                lower[3][:, cols], from_n4[3][:, cols], y_bank[3][:, cols], ALU.min
             )
-            nc.sync.dma_start(out_rows[:, t, cols], result[t][:, cols])
+        for cols in halves:
+            nc.vector.tensor_tensor(
+                result[3][:, cols], upper[3][:, cols], lower[3][:, cols], ALU.subtract
+            )
+            nc.sync.dma_start(out_rows[:, 3, cols], result[3][:, cols])

from contextlib import ExitStack

import concourse.mybir as mybir
from concourse.masks import make_identity

K, T, S, H, N, W = 512, 2048, 512, 512, 512, 256
FLOPS = 2 * K * H * S + 2 * H * N * S

F32 = mybir.dt.float32
BF16 = mybir.dt.bfloat16
I32 = mybir.dt.int32
U32 = mybir.dt.uint32
U16 = mybir.dt.uint16
U8 = mybir.dt.uint8
FP8X4 = mybir.dt.float8_e4m3fn_x4
ALU = mybir.AluOpType
COPY = mybir.ActivationFunctionType.Copy
RELU = mybir.ActivationFunctionType.Relu

P = 128
PACK = 4
QUADRANTS = 4
GROUP = 16
HALF = 256
LAST = PACK - 1


def entries(cols):
    return slice(cols.start // GROUP, cols.stop // GROUP)


def deal_views(dealt, raw, half):
    m = slice(half * P // 2, (half + 1) * P // 2)
    return (
        dealt[:, :, m, :].rearrange("p t m j -> p m j t"),
        raw[:].rearrange("p j (m t) -> p m j t", t=PACK),
    )


def tile_picked_skipmaxbfoldd_none_p_kernel(
    tc, x_words, x_scales, w1, gn, w2, offs, n1, n2, n3, n4, n5, out
):
    nc = tc.nc
    halves = [slice(0, HALF), slice(HALF, 2 * HALF)]
    with ExitStack() as ctx:
        keep = ctx.enter_context(tc.tile_pool(name="keep", bufs=1))
        psum = ctx.enter_context(tc.psum_pool(name="psum", bufs=1))

        def new(shape, dtype, name, tag=""):
            return keep.tile(shape, dtype, name=name, tag=tag or name, align_bytes=64)

        def quantize_weight(dealt, codes, scales):
            nc.vector.quantize_mx(
                out=codes[:].rearrange("p t m -> p (t m)").bitcast(FP8X4),
                scales=scales[:].rearrange("p t m -> p (t m)"),
                in_=dealt[:].rearrange("p t m j -> p (t m j)"),
            )

        def product(result, w_codes, w_scales, codes, scales):
            nc.tensor.matmul_mx(
                out=result,
                lhsT=w_codes.bitcast(FP8X4),
                lhsT_scale=w_scales,
                rhs=codes.bitcast(FP8X4),
                rhs_scale=scales,
                start=True,
                stop=True,
            )

        l_offs = new([P, S // GROUP], U16, "l_offs")
        l_n1 = new([P, W // GROUP], U16, "l_n1")
        l_n2 = new([P, W // GROUP], U16, "l_n2")
        l_n3 = new([P, S // GROUP], U16, "l_n3")
        l_n4 = new([P, S // GROUP], U16, "l_n4")
        l_n5 = new([P, S // GROUP], U16, "l_n5")
        gain = new([P, PACK], F32, "gain")
        table_words = new([P, T], U32, "table_words")
        table_scales = new([P, T], U8, "table_scales")
        w1_raw = [new([P, PACK, HALF], F32, "w1_raw%d" % h) for h in range(2)]
        w2_raw = [new([P, PACK, HALF], F32, "w2_raw%d" % h) for h in range(2)]

        nc.vector.memset(table_scales[:].bitcast(I32), 0)
        scale_rows = new([P, T], U8, "scale_rows")
        live_rows = [slice(32 * q, 32 * q + 4) for q in range(QUADRANTS)]
        w1_rows = w1.rearrange("(p j) c -> p j c", j=PACK)
        w2_rows = w2.rearrange("(p j) c -> p j c", j=PACK)
        nc.sync.dma_start(w1_raw[0][:], w1_rows[:, :, halves[0]])
        for q, rows in enumerate(live_rows):
            nc.sync.dma_start(
                scale_rows[rows, :].bitcast(I32), x_scales[0][4 * q : 4 * q + 4, :].bitcast(I32)
            )
        nc.sync.dma_start(l_offs[:], offs)
        nc.sync.dma_start(w1_raw[1][:], w1_rows[:, :, halves[1]])
        nc.sync.dma_start(
            table_words[:].bitcast(I32), x_words[0].rearrange("p n j -> p (n j)").bitcast(I32)
        )
        nc.sync.dma_start(gain[:], gn.rearrange("(p t) o -> p (t o)", t=PACK))
        nc.sync.dma_start(l_n1[:], n1)
        nc.sync.dma_start(l_n2[:], n2)
        nc.sync.dma_start(l_n3[:], n3)
        for h, cols in enumerate(halves):
            nc.sync.dma_start(w2_raw[h][:], w2_rows[:, :, cols])
        nc.sync.dma_start(l_n5[:], n5)
        nc.sync.dma_start(l_n4[:], n4)

        x_codes = new([P, S], U32, "x_codes")
        x_bytes = new([P, S], U8, "x_bytes")
        for rows in live_rows:
            nc.vector.tensor_copy(
                table_scales[rows, :].bitcast(I32), scale_rows[rows, :].bitcast(I32)
            )
        nc.vector.tensor_copy(x_bytes[:], table_scales[:].indirect(l_offs[:]))

        w1_dealt = new([P, PACK, P, PACK], BF16, "w1_dealt")
        for h in range(2):
            nc.scalar.copy(*deal_views(w1_dealt, w1_raw[h], h))
        w1_codes = new([P, PACK, P], U32, "w1_codes")
        w1_bytes = new([P, PACK, P], U8, "w1_bytes")
        y_bank = [psum.tile([P, S], F32, name="y_bank%d" % t) for t in range(PACK)]
        h_bank = [psum.tile([P, S], F32, name="h_bank%d" % t) for t in range(PACK)]
        ds = [new([P, S], F32, "ds%d" % t) for t in range(PACK)]
        quantize_weight(w1_dealt, w1_codes, w1_bytes)
        for cols in halves:
            nc.vector.tensor_copy(
                x_codes[:, cols], table_words[:].indirect(l_offs[:, entries(cols)])
            )
        y_parts = [(0, halves[0], y_bank[0]), (0, halves[1], h_bank[LAST])]
        y_parts = y_parts + [(t, slice(0, S), y_bank[t]) for t in range(1, PACK)]
        for t, cols, bank in y_parts:
            product(
                bank[:, cols], w1_codes[:, t, :], w1_bytes[:, t, :], x_codes[:, cols], x_bytes[:, cols]
            )
            nc.scalar.activation(ds[t][:, cols], bank[:, cols], COPY, scale=gain[:, t : t + 1])

        pa = [new([P, W], F32, "pa%d" % t) for t in range(PACK)]
        pb_half = [new([P, W], F32, "pb_half%d" % t) for t in range(PACK)]
        ds_half = [new([P, S], F32, "ds_half%d" % t) for t in range(PACK)]
        y_win = [new([P, 2 * S], F32, "y_win%d" % t) for t in range(PACK)]
        h_win = [new([P, 2 * S], F32, "h_win%d" % t) for t in range(PACK)]
        minus_half = new([P, 1], F32, "minus_half", tag="z1")
        nc.gpsimd.memset(minus_half[:], -0.5)

        w2_dealt = new([P, PACK, P, PACK], BF16, "w2_dealt")
        for h in range(2):
            nc.scalar.copy(*deal_views(w2_dealt, w2_raw[h], h))
        for t, cols, bank in y_parts:
            nc.scalar.activation(
                y_win[t][:, cols], bank[:, cols], COPY, scale=-1.0 if t == 0 else 1.0
            )

        identity = new([P, P], F32, "identity")
        make_identity(nc, identity[:])
        blocks = [slice(c * P, (c + 1) * P) for c in range(S // P)]
        sum_bank = psum.tile([P, S], F32, name="sum_bank", tag="y_bank0")

        def add_turned(term, first=False, last=False):
            for block in blocks:
                nc.tensor.matmul(
                    sum_bank[:, block],
                    lhsT=term[:, block],
                    rhs=identity[:],
                    is_transpose=True,
                    start=first and block == blocks[0],
                    stop=last and block == blocks[-1],
                )

        minus_y0 = y_win[0][:, :S]
        add_turned(minus_y0, first=True)

        def fetch_pairs(t):
            nc.vector.tensor_copy(pa[t][:], ds[t][:].indirect(l_n1[:]))
            nc.vector.tensor_scalar(
                pb_half[t][:], ds[t][:].indirect(l_n2[:]), -0.5, 0.0, ALU.mult, ALU.add
            )

        fetch_pairs(0)
        for t in range(PACK):
            if t < LAST:
                fetch_pairs(t + 1)
            nc.vector.tensor_tensor(ds[t][:].indirect(l_n2[:]), pa[t][:], pb_half[t][:], ALU.add)
            nc.scalar.activation(ds_half[t][:], ds[t][:], COPY, scale=minus_half[:])

        z = [new([P, PACK, HALF], F32, "z%d" % h) for h in range(2)]
        for h, cols in enumerate(halves):
            for t in range(PACK):
                nc.vector.tensor_tensor(
                    z[h][:, t, :],
                    ds_half[t][:].indirect(l_n3[:, entries(cols)]),
                    ds[t][:, cols],
                    ALU.add,
                )

        w2_codes = new([P, PACK, P], U32, "w2_codes")
        w2_bytes = new([P, PACK, P], U8, "w2_bytes")
        quantize_weight(w2_dealt, w2_codes, w2_bytes)
        for h, cols in enumerate(halves):
            z_woven = new([P, HALF, PACK], BF16, "z_woven%d" % h)
            z_codes = new([P, HALF], U32, "z_codes%d" % h)
            z_bytes = new([P, HALF], U8, "z_bytes%d" % h)
            nc.scalar.copy(
                z_woven[:].rearrange("p (c i) t -> p c t i", i=4),
                z[h][:].rearrange("p t (c i) -> p c t i", i=4),
            )
            nc.vector.quantize_mx(
                out=z_codes[:].bitcast(FP8X4),
                scales=z_bytes[:],
                in_=z_woven[:].rearrange("p n t -> p (n t)"),
            )
            for t in range(PACK):
                product(
                    h_bank[t][:, cols], w2_codes[:, t, :], w2_bytes[:, t, :], z_codes[:], z_bytes[:]
                )
            nc.scalar.copy(h_win[0][:, cols], h_bank[0][:, cols])

        y5_first = new([P, S], F32, "y5_first", tag="z_woven0")
        y5_rest = new([P, 2, S], F32, "y5_rest", tag="z_woven1")
        y5 = {1: y5_first[:], 2: y5_rest[:, 0, :], 3: y5_rest[:, 1, :]}
        for t in range(1, PACK):
            nc.vector.tensor_copy(y5[t], y_win[t][:].indirect(l_n5[:]))

        out_rows = out.rearrange("(p t) n -> p t n", t=PACK)
        from_n4 = [new([P, S], F32, "from_n4_%d" % t) for t in range(PACK)]
        upper = [new([P, S], F32, "upper%d" % t) for t in range(PACK)]
        lower = [new([P, S], F32, "lower%d" % t) for t in range(PACK)]
        result = [new([P, S], F32, "result%d" % t) for t in range(LAST)] + [upper[2]]

        for t in range(1, PACK):
            nc.scalar.copy(h_win[t][:, :S], h_bank[t][:])

        h0 = h_win[0][:, :S]
        add_turned(h0)
        h_less_y5 = new([P, S], F32, "h_less_y5")
        nc.vector.tensor_tensor(h_less_y5[:], y_win[0][:].indirect(l_n5[:]), h0, ALU.add)
        nc.scalar.activation(upper[0][:], h_less_y5[:], RELU, scale=-1.0)
        add_turned(upper[0])
        nc.vector.tensor_tensor(from_n4[0][:], h_win[0][:].indirect(l_n4[:]), minus_y0, ALU.add)
        nc.scalar.activation(lower[0][:], from_n4[0][:], RELU, scale=-1.0)
        add_turned(lower[0], last=True)

        y1 = y_win[1][:, :S]
        nc.vector.tensor_tensor(from_n4[1][:], h_win[1][:].indirect(l_n4[:]), y1, ALU.subtract)
        nc.vector.tensor_tensor(upper[1][:], y5[1], h_bank[1][:], ALU.max)
        nc.scalar.activation(lower[1][:], from_n4[1][:], RELU, scale=-1.0)
        upper_less_y = new([P, S], F32, "upper_less_y")
        nc.gpsimd.tensor_tensor(upper_less_y[:], upper[1][:], y1, ALU.subtract)
        nc.gpsimd.tensor_tensor(result[1][:], upper_less_y[:], lower[1][:], ALU.add)
        nc.sync.dma_start(out_rows[:, 1, :], result[1][:])

        turned = new([P, S], F32, "turned")
        nc.scalar.copy(turned[:], sum_bank[:])
        back_bank = psum.tile([P, S], F32, name="back_bank", tag="h_bank0")
        for block in blocks:
            nc.tensor.transpose(back_bank[:, block], turned[:, block], identity[:])
        nc.scalar.copy(result[0][:], back_bank[:])
        nc.scalar.dma_start(out_rows[:, 0, :], result[0][:])

        nc.vector.tensor_copy(from_n4[2][:], h_win[2][:].indirect(l_n4[:]))
        nc.vector.tensor_tensor(upper[2][:], y5[2], h_bank[2][:], ALU.max)
        nc.vector.tensor_tensor(lower[2][:], from_n4[2][:], y_bank[2][:], ALU.min)
        nc.gpsimd.tensor_tensor(result[2][:], upper[2][:], lower[2][:], ALU.subtract)
        nc.sync.dma_start(out_rows[:, 2, :], result[2][:])

        nc.vector.tensor_copy(from_n4[3][:], h_win[3][:].indirect(l_n4[:]))
        nc.vector.tensor_tensor(upper[3][:], y5[3], h_bank[3][:], ALU.max)
        for cols in halves:
            nc.vector.tensor_tensor(
                lower[3][:, cols], from_n4[3][:, cols], y_bank[3][:, cols], ALU.min
            )
        for cols in halves:
            nc.vector.tensor_tensor(
                result[3][:, cols], upper[3][:, cols], lower[3][:, cols], ALU.subtract
            )
            nc.sync.dma_start(out_rows[:, 3, cols], result[3][:, cols])
